import numpy as np
import ml_dtypes


def mxq(x, axis, fmt="e4m3"):
    dtype, down = {"e4m3": (ml_dtypes.float8_e4m3fn, 7), "e5m2": (ml_dtypes.float8_e5m2, 14)}[fmt]
    v = np.moveaxis(np.asarray(x, np.float32).astype(ml_dtypes.bfloat16).astype(np.float64), axis, -1)
    blocks = v.reshape(v.shape[:-1] + (-1, 32))
    amax = np.abs(blocks).max(-1, keepdims=True)
    byte = np.maximum(np.where(amax > 0, np.frexp(amax)[1] - 1 + 127, 0) - down, 1)
    scale = np.exp2(byte - 127.0)
    codes = (blocks / scale).astype(np.float32).astype(dtype).astype(np.float64)
    return np.moveaxis((codes * scale).reshape(v.shape), -1, axis)


WIDE = False


def mx_kscale(k):
    if not WIDE:
        return np.ones(k)
    levels = np.array([10, -10, 5, -5, 0])
    if k % 512:
        return np.exp2(np.random.permutation(np.resize(levels, k // 32))).repeat(32)
    a = np.empty((k // 512, 16))
    for p in range(k // 512):
        a[p, :8] = np.random.permutation(np.resize(levels, 8))
        for g in range(8):
            far = levels[np.abs(levels - a[p, g]) >= 10]
            a[p, g + 8] = far[np.random.randint(len(far))]
    return np.exp2(a.ravel()).repeat(32)


BF16 = ml_dtypes.bfloat16


def bf(x):
    return np.asarray(x, np.float32).astype(BF16)


def f64(x):
    return np.asarray(x).astype(np.float64)


E2M1 = np.array([0.0, 0.5, 1.0, 1.5, 2.0, 3.0, 4.0, 6.0, -0.0, -0.5, -1.0, -1.5, -2.0, -3.0, -4.0, -6.0])


def pack_weight(w, fmt):
    k, n = w.shape
    w = f64(bf(w)).reshape(k // 32, 32, n)
    amax = np.abs(w).max(1)
    if fmt == "e4m3":
        byte = np.frexp(amax)[1] - 1 + 127 - 7
    else:
        mant, ex = np.frexp(amax / 6.0)
        byte = np.where(mant > 0.5, ex, ex - 1) + 127
    byte = np.clip(np.where(amax > 0, byte, 1), 1, 254)
    scaled = (w * np.exp2(127.0 - byte)[:, None, :]).reshape(k, n).astype(np.float32)
    by_word = np.ascontiguousarray(scaled.reshape(k // 512, 128, 4, n).transpose(0, 1, 3, 2))
    if fmt == "e4m3":
        words = by_word.astype(ml_dtypes.float8_e4m3fn).view(np.uint8)
    else:
        c = by_word.astype(ml_dtypes.float4_e2m1fn).view(np.uint8) & 0xF
        words = c[..., 0::2] | (c[..., 1::2] << 4)
    return np.ascontiguousarray(words), np.ascontiguousarray(byte.astype(np.uint8).reshape(k // 512, 16, n))


def unpack_weight(words, scales, fmt):
    g, p, n, _ = words.shape
    if fmt == "e4m3":
        vals = np.ascontiguousarray(words).view(ml_dtypes.float8_e4m3fn).astype(np.float64)
    else:
        nib = np.empty((g, p, n, 4), np.uint8)
        nib[..., 0::2] = words & 0xF
        nib[..., 1::2] = words >> 4
        vals = E2M1[nib]
    vals = vals * np.repeat(np.exp2(scales.astype(np.float64) - 127.0), 8, axis=1)[..., None]
    return vals.transpose(0, 1, 3, 2).reshape(g * 512, n)
def pack4(w):
    words, scales = pack_weight(w, "e2m1")
    return words.reshape(words.shape[0], 128, -1), scales


def unpack4(words, scales):
    return unpack_weight(words.reshape(words.shape[0], 128, -1, 2), scales, "e2m1")


G, B, P, Q, V = 3, 1024, 1024, 1024, 512

FLOOR = 0.05
GAMMA = 2.2


def setup_inputs():
    s, t = mx_kscale(G * P), mx_kscale(G * Q)
    patterns = np.random.standard_normal((G, B, P)) + 2.0 / np.sqrt(P)
    transport = np.random.standard_normal((G * P, Q)) ** 2 / np.sqrt(3.0 * P)
    gain = 1.0 + 0.1 * np.random.standard_normal((G, Q))
    encoder = np.random.standard_normal((G * Q, V)) / np.sqrt(Q)
    transport_words, transport_scales = pack4(transport / s[:, None])
    encoder_words, encoder_scales = pack4(encoder / t[:, None])
    return {"patterns": bf(patterns * s.reshape(G, 1, P)),
            "transport_words": transport_words, "transport_scales": transport_scales,
            "gain": bf(gain * t.reshape(G, Q)),
            "encoder_words": encoder_words, "encoder_scales": encoder_scales}


def reference(patterns, transport_words, transport_scales, gain, encoder_words, encoder_scales):
    transport = unpack4(transport_words, transport_scales).reshape(G, P, Q)
    encoder = unpack4(encoder_words, encoder_scales).reshape(G, Q, V)
    dual = mxq(f64(patterns), 2, "e4m3") @ transport
    corrected = np.maximum(dual, FLOOR) ** (1.0 / GAMMA) * f64(gain)[:, None, :]
    return mxq(corrected, 2, "e4m3") @ encoder

@@ -1,0 +1,307 @@
+from contextlib import ExitStack
+
+import concourse.mybir as mybir
+from concourse.masks import make_identity
+
+F32 = mybir.dt.float32
+BF16 = mybir.dt.bfloat16
+I32 = mybir.dt.int32
+U32 = mybir.dt.uint32
+U8 = mybir.dt.uint8
+E4M3 = mybir.dt.float8_e4m3fn_x4
+E2M1 = mybir.dt.float4_e2m1fn_x4
+ALU = mybir.AluOpType
+ACT = mybir.ActivationFunctionType
+
+G, B, P, Q, V = 3, 1024, 1024, 1024, 512
+FLOPS = 2 * G * B * (P * Q + Q * V)
+BLACK = 0.05
+GAMMA = 2.2
+N = 512
+RT = 4
+UNITS = [(c, h) for c in range(G) for h in range(2)]
+LAST = len(UNITS) - 1
+
+PERM = "VGG"
+EVAC = ["SSSS", "SSSV", "VSVV", "SSVV", "VVVV", "VVVV"]
+OUT = ["VVVV", "VVVV", "VVSS", "SVSV", "SSSS", "SSSV"]
+FIRST = 2
+GPSIGN = 2
+
+
+def tile_dual_photo_gamma_encode_s14_kernel(
+    tc, patterns, transport_words, transport_scales, gain, encoder_words, encoder_scales, out
+):
+    nc = tc.nc
+
+    with ExitStack() as ctx:
+        keep = ctx.enter_context(tc.tile_pool(name="keep", bufs=1))
+        work = ctx.enter_context(tc.tile_pool(name="work", bufs=2))
+        psum = ctx.enter_context(tc.psum_pool(name="psum", bufs=8))
+        ctx.enter_context(tc.manual_schedule())
+
+        def copy(engine, dst, src):
+            if engine == "S":
+                nc.scalar.copy(out=dst, in_=src)
+            else:
+                nc.vector.tensor_copy(out=dst, in_=src)
+
+        t_planes = keep.tile([128, 6 * 1024], U8, align_bytes=64)
+        e_planes = keep.tile([128, 6 * 512], U8, align_bytes=64)
+        nc.vector.memset(t_planes[:, 0:2048].bitcast(I32), 0)
+        nc.vector.memset(t_planes[:, 2048:6144].bitcast(I32), 0)
+        nc.vector.memset(e_planes[:].bitcast(I32), 0)
+        ident = keep.tile([128, 128], F32)
+        make_identity(nc, ident[:])
+
+        gain_raw = keep.tile([128, 24], BF16)
+        nc.scalar.dma_start(
+            out=gain_raw[:].rearrange("p (s t) -> p s t", t=4),
+            in_=gain.rearrange("c (u p t) -> p (c u) t", p=128, t=4),
+        )
+
+        def load_scales(planes, scales, g0, g1, width):
+            for r in range(4):
+                nc.sync.dma_start(
+                    out=planes[r:128:32, width * g0 : width * g1].bitcast(I32).rearrange("q (g n) -> q g n", g=g1 - g0),
+                    in_=scales[g0:g1, r::4, :].bitcast(I32).rearrange("g q n -> q g n"),
+                )
+
+        pats = {}
+
+        def load_patterns(u, pieces):
+            c, h = UNITS[u]
+            pat = work.tile([128, RT, 1024], BF16, name="pat", tag="io", bufs=3)
+            src = patterns[c, N * h : N * (h + 1), :].rearrange("(p r) k -> p r k", r=RT)
+            step = RT // pieces
+            for i in range(pieces):
+                nc.sync.dma_start(out=pat[:, i * step : (i + 1) * step, :], in_=src[:, i * step : (i + 1) * step, :])
+            pats[u] = pat
+
+        traws = {}
+
+        def load_transport(c):
+            traw = work.tile([128, 2 * 2048], U8, name="traw")
+            for g in range(2):
+                nc.sync.dma_start(
+                    out=traw[:, 2048 * g : 2048 * (g + 1)].bitcast(I32), in_=transport_words[2 * c + g].bitcast(I32)
+                )
+            traws[c] = traw
+
+        load_scales(t_planes, transport_scales, 0, 2, 1024)
+        load_transport(0)
+        load_patterns(0, 4)
+        load_patterns(1, 4)
+        load_scales(t_planes, transport_scales, 2, 6, 1024)
+        load_transport(1)
+        load_patterns(2, 2)
+        load_scales(e_planes, encoder_scales, 0, 6, 512)
+        e_words = keep.tile([128, 6 * 1024], U8, align_bytes=64)
+
+        def load_encoder():
+            for g in range(6):
+                nc.sync.dma_start(
+                    out=e_words[:, 1024 * g : 1024 * (g + 1)].bitcast(I32), in_=encoder_words[g].bitcast(I32)
+                )
+
+        gain_f = keep.tile([128, 24], F32)
+        nc.vector.tensor_copy(out=gain_f[:], in_=gain_raw[:])
+        frac = keep.tile([128, 24], F32)
+        nc.vector.tensor_scalar(
+            out=frac[:].bitcast(I32), in0=gain_f[:].bitcast(I32), scalar1=0x7FFFFF, scalar2=0x3F800000,
+            op0=ALU.bitwise_and, op1=ALU.bitwise_or,
+        )
+        power = keep.tile([128, 24], F32)
+        nc.vector.tensor_scalar(
+            out=power[:].bitcast(I32), in0=gain_f[:].bitcast(I32), scalar1=23, scalar2=23,
+            op0=ALU.logical_shift_right, op1=ALU.logical_shift_left,
+        )
+        expo = keep.tile([128, 24], F32)
+        nc.vector.tensor_scalar(out=expo[:], in0=frac[:], scalar1=0.0, scalar2=GAMMA, op0=ALU.mult, op1=ALU.add)
+        signs = keep.tile([128, 24], BF16)
+        nc.vector.tensor_copy(out=signs[:], in_=power[:])
+        lift = keep.tile([128, 24], F32)
+        for c in range(G):
+            cols = slice(8 * c, 8 * (c + 1))
+            nc.gpsimd.tensor_tensor(out=lift[:, cols], in0=frac[:, cols], in1=expo[:, cols], op=ALU.pow)
+
+        tcodes = {}
+
+        def permute_transport(c):
+            eng = nc.vector if PERM[c] == "V" else nc.gpsimd
+            codes = work.tile([128, 16, 256], U8, align_bytes=64, name="codes")
+            scales = work.tile([128, 2, 2, 4, 128], U8, align_bytes=64, name="scales")
+            for h in range(2):
+                for g in range(2):
+                    i = 2 * g + h
+                    eng.tensor_copy(
+                        out=codes[:, 4 * i : 4 * (i + 1), :].rearrange("p t (m b) -> p t m b", b=2),
+                        in_=traws[c][:, 1024 * i : 1024 * (i + 1)].rearrange("p (m t b) -> p t m b", t=4, b=2),
+                    )
+                eng.tensor_copy(
+                    out=scales[:, :, h],
+                    in_=t_planes[:, 2048 * c : 2048 * (c + 1)].rearrange("p (g h m t) -> p h g t m", g=2, h=2, t=4)[:, h],
+                )
+            tcodes[c] = (codes, scales)
+
+        xs, pq = {}, {}
+
+        def turn(u, rt):
+            if rt == 0:
+                x = work.tile([128, 2, N * 4], BF16, align_bytes=64, name="x", tag="quad", bufs=5)
+                xs[u] = x
+            xw = xs[u][:].rearrange("p g w -> p (g w)").bitcast(F32).rearrange("p (g r e) -> p g r e", g=2, e=2)
+            tp = psum.tile([128, 4, 128], F32, name="tp", tag="bank")
+            words = pats[u][:, rt, :].bitcast(F32)
+            for g in range(2):
+                for e in range(2):
+                    nc.tensor.transpose(tp[:, 2 * g + e, :], words[:, 256 * g + e : 256 * (g + 1) : 2], ident[:])
+            copy(EVAC[u][rt], xw[:, :, 128 * rt : 128 * (rt + 1), :], tp[:].rearrange("p (g e) r -> p g r e", g=2))
+
+        def quantize_patterns(u, g):
+            if g == 0:
+                codes = work.tile([128, 2, N], U32, align_bytes=64, name="qcodes", tag="qcodes", bufs=4)
+                scales = work.tile([128, 2, N], U8, align_bytes=64, name="qscales", tag="qscales", bufs=4)
+                pq[u] = (codes, scales)
+            codes, scales = pq[u]
+            nc.vector.quantize_mx(out=codes[:, g, :].bitcast(E4M3), scales=scales[:, g, :], in_=xs[u][:, g, :])
+
+        ms, ls = {}, {}
+
+        def stage1(u, h, t):
+            c = UNITS[u][0]
+            tcode, tscale = tcodes[c]
+            codes, scales = pq[u]
+            if t == 0:
+                m = work.tile([128, 4, N], F32, name="m", bufs=5)
+                ms[u, h] = m
+            acc = psum.tile([128, N], F32, name="acc", tag="bank")
+            for g in range(2):
+                nc.tensor.matmul_mx(
+                    out=acc[:], lhsT=tcode[:, 8 * g + 4 * h + t, :].bitcast(E2M1), lhsT_scale=tscale[:, g, h, t],
+                    rhs=codes[:, g, :].bitcast(E4M3), rhs_scale=scales[:, g, :], start=g == 0, stop=g == 1,
+                )
+            col = 8 * c + 4 * h + t
+            nc.vector.tensor_scalar(
+                out=ms[u, h][:, t, :], in0=acc[:], scalar1=BLACK, scalar2=lift[:, col : col + 1],
+                op0=ALU.max, op1=ALU.mult,
+            )
+
+        def log(u, h):
+            lg = work.tile([128, 2, N, 2], F32, name="lg", bufs=8)
+            nc.scalar.activation(out=lg[:], in_=ms[u, h][:].rearrange("p (q e) n -> p q n e", e=2), func=ACT.Ln)
+            ls[u, h] = lg
+
+        ys, cq = {}, {}
+
+        def exp(u, h, r0, r1):
+            if h == 0 and r0 == 0:
+                y = work.tile([128, 2, N, 4], BF16, align_bytes=64, name="y", tag="quad", bufs=5)
+                ys[u] = y
+            nc.scalar.activation(
+                out=ys[u][:, h, r0:r1].rearrange("p n (q e) -> p n q e", e=2),
+                in_=ls[u, h][:, :, r0:r1].rearrange("p q n e -> p n q e"), func=ACT.Exp, scale=1.0 / GAMMA,
+            )
+
+        def sign(eng, u, h, r0, r1):
+            col = 8 * UNITS[u][0] + 4 * h
+            y = ys[u][:, h, r0:r1]
+            eng.tensor_tensor(
+                out=y, in0=y, in1=signs[:, col : col + 4].unsqueeze(1).to_broadcast([128, r1 - r0, 4]), op=ALU.mult
+            )
+
+        def quantize_corrected(u, h, r0, r1):
+            if h == 0 and r0 == 0:
+                codes = work.tile([128, 2, N], U32, align_bytes=64, name="qcodes", tag="qcodes", bufs=4)
+                scales = work.tile([128, 2, N], U8, align_bytes=64, name="qscales", tag="qscales", bufs=4)
+                cq[u] = (codes, scales)
+            codes, scales = cq[u]
+            nc.vector.quantize_mx(
+                out=codes[:, h, r0:r1].bitcast(E4M3), scales=scales[:, h, r0:r1],
+                in_=ys[u][:, h, r0:r1].rearrange("p n t -> p (n t)"),
+            )
+
+        outs = {}
+
+        def stage2(u, rt, stores):
+            c, h = UNITS[u]
+            codes, scales = cq[u]
+            if rt == 0:
+                o = work.tile([128, RT, V], F32, name="o", tag="io", bufs=3)
+                outs[u] = o
+            acc = psum.tile([128, V], F32, name="oacc", tag="bank")
+            cols = slice(128 * rt, 128 * (rt + 1))
+            for g in range(2):
+                k = 2 * c + g
+                nc.tensor.matmul_mx(
+                    out=acc[:], lhsT=codes[:, g, cols].bitcast(E4M3), lhsT_scale=scales[:, g, cols],
+                    rhs=e_words[:, 1024 * k : 1024 * (k + 1)].bitcast(E2M1),
+                    rhs_scale=e_planes[:, 512 * k : 512 * (k + 1)], start=g == 0, stop=g == 1,
+                )
+            copy(OUT[u][rt], outs[u][:, rt, :], acc[:])
+            if (rt + 1) % stores == 0:
+                rows = slice(rt + 1 - stores, rt + 1)
+                nc.sync.dma_start(
+                    out=out[c, N * h : N * (h + 1), :].rearrange("(p r) v -> p r v", r=RT)[:, rows, :],
+                    in_=outs[u][:, rows, :],
+                )
+
+        permute_transport(0)
+        for rt in range(RT):
+            turn(0, rt)
+        quantize_patterns(0, 0)
+        quantize_patterns(0, 1)
+        for rt in range(RT):
+            turn(1, rt)
+        permute_transport(1)
+        load_transport(2)
+        load_patterns(3, 2)
+        load_encoder()
+        for u in range(LAST + 1):
+            if u == 2:
+                permute_transport(2)
+            for h in range(2):
+                for t in range(4):
+                    stage1(u, h, t)
+                    if u == 0 and h == 0 and t % 2:
+                        quantize_patterns(1, t // 2)
+                log(u, h)
+                if u + 2 <= LAST:
+                    turn(u + 2, 2 * h)
+                    turn(u + 2, 2 * h + 1)
+            if u + 2 <= LAST:
+                quantize_patterns(u + 2, 0)
+                quantize_patterns(u + 2, 1)
+            if u + 4 <= LAST:
+                load_patterns(u + 4, 2)
+            if u == FIRST - 1:
+                for v in range(FIRST):
+                    for h in range(2):
+                        exp(v, h, 0, N)
+                        if v < GPSIGN:
+                            sign(nc.gpsimd, v, h, 0, N)
+        for u in range(FIRST, LAST):
+            for h in range(2):
+                exp(u, h, 0, N)
+        for u in range(LAST):
+            for h in range(2):
+                if u >= GPSIGN:
+                    sign(nc.vector, u, h, 0, N)
+                if u:
+                    stage2(u - 1, h, 2)
+            for h in range(2):
+                quantize_corrected(u, h, 0, N)
+                if u:
+                    stage2(u - 1, 2 + h, 2)
+        for rt in range(RT):
+            for h in range(2):
+                exp(LAST, h, 128 * rt, 128 * (rt + 1))
+        for rt in range(RT + 1):
+            if rt < RT:
+                stage2(LAST - 1, rt, 2)
+                for h in range(2):
+                    sign(nc.vector, LAST, h, 128 * rt, 128 * (rt + 1))
+            if rt:
+                for h in range(2):
+                    quantize_corrected(LAST, h, 128 * (rt - 1), 128 * rt)
+                stage2(LAST, rt - 1, 1)

@@ -23,10 +23,12 @@ UNITS = [(c, h) for c in range(G) for h in range(2)]
 LAST = len(UNITS) - 1
 
 PERM = "VGG"
-EVAC = ["SSSS", "SSSV", "VSVV", "SSVV", "VVVV", "VVVV"]
-OUT = ["VVVV", "VVVV", "VVSS", "SVSV", "SSSS", "SSSV"]
+EVAC = ["VSSS", "SSSS", "SSVV", "SSVV", "VVVV", "VVVV"]
+OUT = ["VVVV", "VVVV", "VSVS", "VSVS", "SSSS", "SSSV"]
 FIRST = 2
-GPSIGN = 2
+GPSIGN = 0
+PERMAT = {1: 1, 2: 2}
+SIGNCHUNK = 512
 
 
 def tile_dual_photo_gamma_encode_s14_kernel(
@@ -49,10 +51,10 @@ def tile_dual_photo_gamma_encode_s14_kernel(
         t_planes = keep.tile([128, 6 * 1024], U8, align_bytes=64)
         e_planes = keep.tile([128, 6 * 512], U8, align_bytes=64)
         nc.vector.memset(t_planes[:, 0:2048].bitcast(I32), 0)
-        nc.vector.memset(t_planes[:, 2048:6144].bitcast(I32), 0)
-        nc.vector.memset(e_planes[:].bitcast(I32), 0)
         ident = keep.tile([128, 128], F32)
         make_identity(nc, ident[:])
+        nc.gpsimd.memset(t_planes[:, 2048:6144].bitcast(I32), 0)
+        nc.gpsimd.memset(e_planes[:].bitcast(I32), 0)
 
         gain_raw = keep.tile([128, 24], BF16)
         nc.scalar.dma_start(
@@ -60,9 +62,9 @@ def tile_dual_photo_gamma_encode_s14_kernel(
             in_=gain.rearrange("c (u p t) -> p (c u) t", p=128, t=4),
         )
 
-        def load_scales(planes, scales, g0, g1, width):
+        def load_scales(queue, planes, scales, g0, g1, width):
             for r in range(4):
-                nc.sync.dma_start(
+                queue.dma_start(
                     out=planes[r:128:32, width * g0 : width * g1].bitcast(I32).rearrange("q (g n) -> q g n", g=g1 - g0),
                     in_=scales[g0:g1, r::4, :].bitcast(I32).rearrange("g q n -> q g n"),
                 )
@@ -80,22 +82,24 @@ def tile_dual_photo_gamma_encode_s14_kernel(
 
         traws = {}
 
-        def load_transport(c):
-            traw = work.tile([128, 2 * 2048], U8, name="traw")
-            for g in range(2):
-                nc.sync.dma_start(
-                    out=traw[:, 2048 * g : 2048 * (g + 1)].bitcast(I32), in_=transport_words[2 * c + g].bitcast(I32)
-                )
-            traws[c] = traw
+        def load_transport(c, pieces):
+            if c not in traws:
+                traws[c] = work.tile([128, 2, 2048], U8, name="traw")
+            for lo, hi in pieces:
+                for g in range(2):
+                    nc.sync.dma_start(
+                        out=traws[c][:, g, lo:hi].bitcast(I32), in_=transport_words[2 * c + g, :, lo:hi].bitcast(I32)
+                    )
 
-        load_scales(t_planes, transport_scales, 0, 2, 1024)
-        load_transport(0)
+        load_scales(nc.scalar, t_planes, transport_scales, 0, 2, 1024)
+        load_transport(0, [(0, 1024)])
         load_patterns(0, 4)
+        load_transport(0, [(1024, 2048)])
         load_patterns(1, 4)
-        load_scales(t_planes, transport_scales, 2, 6, 1024)
-        load_transport(1)
+        load_scales(nc.sync, t_planes, transport_scales, 2, 6, 1024)
+        load_transport(1, [(0, 2048)])
         load_patterns(2, 2)
-        load_scales(e_planes, encoder_scales, 0, 6, 512)
+        load_scales(nc.sync, e_planes, encoder_scales, 0, 6, 512)
         e_words = keep.tile([128, 6 * 1024], U8, align_bytes=64)
 
         def load_encoder():
@@ -105,44 +109,49 @@ def tile_dual_photo_gamma_encode_s14_kernel(
                 )
 
         gain_f = keep.tile([128, 24], F32)
-        nc.vector.tensor_copy(out=gain_f[:], in_=gain_raw[:])
         frac = keep.tile([128, 24], F32)
-        nc.vector.tensor_scalar(
-            out=frac[:].bitcast(I32), in0=gain_f[:].bitcast(I32), scalar1=0x7FFFFF, scalar2=0x3F800000,
-            op0=ALU.bitwise_and, op1=ALU.bitwise_or,
-        )
         power = keep.tile([128, 24], F32)
-        nc.vector.tensor_scalar(
-            out=power[:].bitcast(I32), in0=gain_f[:].bitcast(I32), scalar1=23, scalar2=23,
-            op0=ALU.logical_shift_right, op1=ALU.logical_shift_left,
-        )
         expo = keep.tile([128, 24], F32)
-        nc.vector.tensor_scalar(out=expo[:], in0=frac[:], scalar1=0.0, scalar2=GAMMA, op0=ALU.mult, op1=ALU.add)
         signs = keep.tile([128, 24], BF16)
-        nc.vector.tensor_copy(out=signs[:], in_=power[:])
         lift = keep.tile([128, 24], F32)
-        for c in range(G):
-            cols = slice(8 * c, 8 * (c + 1))
-            nc.gpsimd.tensor_tensor(out=lift[:, cols], in0=frac[:, cols], in1=expo[:, cols], op=ALU.pow)
+
+        def split_gain():
+            nc.vector.tensor_copy(out=gain_f[:], in_=gain_raw[:])
+            nc.vector.tensor_scalar(
+                out=frac[:].bitcast(I32), in0=gain_f[:].bitcast(I32), scalar1=0x7FFFFF, scalar2=0x3F800000,
+                op0=ALU.bitwise_and, op1=ALU.bitwise_or,
+            )
+            nc.vector.tensor_scalar(
+                out=power[:].bitcast(I32), in0=gain_f[:].bitcast(I32), scalar1=23, scalar2=23,
+                op0=ALU.logical_shift_right, op1=ALU.logical_shift_left,
+            )
+            nc.vector.tensor_scalar(out=expo[:], in0=frac[:], scalar1=0.0, scalar2=GAMMA, op0=ALU.mult, op1=ALU.add)
+            nc.vector.tensor_copy(out=signs[:], in_=power[:])
+            for c in range(G):
+                cols = slice(8 * c, 8 * (c + 1))
+                nc.gpsimd.tensor_tensor(out=lift[:, cols], in0=frac[:, cols], in1=expo[:, cols], op=ALU.pow)
 
         tcodes = {}
 
-        def permute_transport(c):
+        def permute_transport(c, h):
             eng = nc.vector if PERM[c] == "V" else nc.gpsimd
-            codes = work.tile([128, 16, 256], U8, align_bytes=64, name="codes")
-            scales = work.tile([128, 2, 2, 4, 128], U8, align_bytes=64, name="scales")
-            for h in range(2):
-                for g in range(2):
-                    i = 2 * g + h
-                    eng.tensor_copy(
-                        out=codes[:, 4 * i : 4 * (i + 1), :].rearrange("p t (m b) -> p t m b", b=2),
-                        in_=traws[c][:, 1024 * i : 1024 * (i + 1)].rearrange("p (m t b) -> p t m b", t=4, b=2),
-                    )
+            if h == 0:
+                codes = work.tile([128, 16, 256], U8, align_bytes=64, name="codes")
+                scales = work.tile([128, 2, 2, 4, 128], U8, align_bytes=64, name="scales")
+                tcodes[c] = (codes, scales)
+            codes, scales = tcodes[c]
+            for g in range(2):
+                i = 2 * g + h
                 eng.tensor_copy(
-                    out=scales[:, :, h],
-                    in_=t_planes[:, 2048 * c : 2048 * (c + 1)].rearrange("p (g h m t) -> p h g t m", g=2, h=2, t=4)[:, h],
+                    out=codes[:, 4 * i : 4 * (i + 1), :].rearrange("p t (m b) -> p t m b", b=2),
+                    in_=traws[c][:, g, 1024 * h : 1024 * (h + 1)].rearrange("p (m t b) -> p t m b", t=4, b=2),
                 )
-            tcodes[c] = (codes, scales)
+            if c == 0 and h == 0:
+                split_gain()
+            eng.tensor_copy(
+                out=scales[:, :, h],
+                in_=t_planes[:, 2048 * c : 2048 * (c + 1)].rearrange("p (g h m t) -> p h g t m", g=2, h=2, t=4)[:, h],
+            )
 
         xs, pq = {}, {}
 
@@ -246,20 +255,22 @@ def tile_dual_photo_gamma_encode_s14_kernel(
                     in_=outs[u][:, rows, :],
                 )
 
-        permute_transport(0)
         for rt in range(RT):
             turn(0, rt)
+        permute_transport(0, 0)
         quantize_patterns(0, 0)
         quantize_patterns(0, 1)
+        permute_transport(0, 1)
         for rt in range(RT):
             turn(1, rt)
-        permute_transport(1)
-        load_transport(2)
+        load_transport(2, [(0, 2048)])
         load_patterns(3, 2)
         load_encoder()
         for u in range(LAST + 1):
-            if u == 2:
-                permute_transport(2)
+            if u in PERMAT:
+                c = PERMAT[u]
+                permute_transport(c, 0)
+                permute_transport(c, 1)
             for h in range(2):
                 for t in range(4):
                     stage1(u, h, t)
@@ -279,7 +290,8 @@ def tile_dual_photo_gamma_encode_s14_kernel(
                     for h in range(2):
                         exp(v, h, 0, N)
                         if v < GPSIGN:
-                            sign(nc.gpsimd, v, h, 0, N)
+                            for r0 in range(0, N, SIGNCHUNK):
+                                sign(nc.gpsimd, v, h, r0, r0 + SIGNCHUNK)
         for u in range(FIRST, LAST):
             for h in range(2):
                 exp(u, h, 0, N)

from contextlib import ExitStack

import concourse.mybir as mybir
from concourse.masks import make_identity

F32 = mybir.dt.float32
BF16 = mybir.dt.bfloat16
I32 = mybir.dt.int32
U32 = mybir.dt.uint32
U8 = mybir.dt.uint8
E4M3 = mybir.dt.float8_e4m3fn_x4
E2M1 = mybir.dt.float4_e2m1fn_x4
ALU = mybir.AluOpType
ACT = mybir.ActivationFunctionType

G, B, P, Q, V = 3, 1024, 1024, 1024, 512
FLOPS = 2 * G * B * (P * Q + Q * V)
BLACK = 0.05
GAMMA = 2.2
N = 512
RT = 4
UNITS = [(c, h) for c in range(G) for h in range(2)]
LAST = len(UNITS) - 1

PERM = "VGG"
EVAC = ["VSSS", "SSSS", "SSVV", "SSVV", "VVVV", "VVVV"]
OUT = ["VVVV", "VVVV", "VSVS", "VSVS", "SSSS", "SSSV"]
FIRST = 2
GPSIGN = 0
PERMAT = {1: 1, 2: 2}
SIGNCHUNK = 512


def tile_dual_photo_gamma_encode_s14_kernel(
    tc, patterns, transport_words, transport_scales, gain, encoder_words, encoder_scales, out
):
    nc = tc.nc

    with ExitStack() as ctx:
        keep = ctx.enter_context(tc.tile_pool(name="keep", bufs=1))
        work = ctx.enter_context(tc.tile_pool(name="work", bufs=2))
        psum = ctx.enter_context(tc.psum_pool(name="psum", bufs=8))
        ctx.enter_context(tc.manual_schedule())

        def copy(engine, dst, src):
            if engine == "S":
                nc.scalar.copy(out=dst, in_=src)
            else:
                nc.vector.tensor_copy(out=dst, in_=src)

        t_planes = keep.tile([128, 6 * 1024], U8, align_bytes=64)
        e_planes = keep.tile([128, 6 * 512], U8, align_bytes=64)
        nc.vector.memset(t_planes[:, 0:2048].bitcast(I32), 0)
        ident = keep.tile([128, 128], F32)
        make_identity(nc, ident[:])
        nc.gpsimd.memset(t_planes[:, 2048:6144].bitcast(I32), 0)
        nc.gpsimd.memset(e_planes[:].bitcast(I32), 0)

        gain_raw = keep.tile([128, 24], BF16)
        nc.scalar.dma_start(
            out=gain_raw[:].rearrange("p (s t) -> p s t", t=4),
            in_=gain.rearrange("c (u p t) -> p (c u) t", p=128, t=4),
        )

        def load_scales(queue, planes, scales, g0, g1, width):
            for r in range(4):
                queue.dma_start(
                    out=planes[r:128:32, width * g0 : width * g1].bitcast(I32).rearrange("q (g n) -> q g n", g=g1 - g0),
                    in_=scales[g0:g1, r::4, :].bitcast(I32).rearrange("g q n -> q g n"),
                )

        pats = {}

        def load_patterns(u, pieces):
            c, h = UNITS[u]
            pat = work.tile([128, RT, 1024], BF16, name="pat", tag="io", bufs=3)
            src = patterns[c, N * h : N * (h + 1), :].rearrange("(p r) k -> p r k", r=RT)
            step = RT // pieces
            for i in range(pieces):
                nc.sync.dma_start(out=pat[:, i * step : (i + 1) * step, :], in_=src[:, i * step : (i + 1) * step, :])
            pats[u] = pat

        traws = {}

        def load_transport(c, pieces):
            if c not in traws:
                traws[c] = work.tile([128, 2, 2048], U8, name="traw")
            for lo, hi in pieces:
                for g in range(2):
                    nc.sync.dma_start(
                        out=traws[c][:, g, lo:hi].bitcast(I32), in_=transport_words[2 * c + g, :, lo:hi].bitcast(I32)
                    )

        load_scales(nc.scalar, t_planes, transport_scales, 0, 2, 1024)
        load_transport(0, [(0, 1024)])
        load_patterns(0, 4)
        load_transport(0, [(1024, 2048)])
        load_patterns(1, 4)
        load_scales(nc.sync, t_planes, transport_scales, 2, 6, 1024)
        load_transport(1, [(0, 2048)])
        load_patterns(2, 2)
        load_scales(nc.sync, e_planes, encoder_scales, 0, 6, 512)
        e_words = keep.tile([128, 6 * 1024], U8, align_bytes=64)

        def load_encoder():
            for g in range(6):
                nc.sync.dma_start(
                    out=e_words[:, 1024 * g : 1024 * (g + 1)].bitcast(I32), in_=encoder_words[g].bitcast(I32)
                )

        gain_f = keep.tile([128, 24], F32)
        frac = keep.tile([128, 24], F32)
        power = keep.tile([128, 24], F32)
        expo = keep.tile([128, 24], F32)
        signs = keep.tile([128, 24], BF16)
        lift = keep.tile([128, 24], F32)

        def split_gain():
            nc.vector.tensor_copy(out=gain_f[:], in_=gain_raw[:])
            nc.vector.tensor_scalar(
                out=frac[:].bitcast(I32), in0=gain_f[:].bitcast(I32), scalar1=0x7FFFFF, scalar2=0x3F800000,
                op0=ALU.bitwise_and, op1=ALU.bitwise_or,
            )
            nc.vector.tensor_scalar(
                out=power[:].bitcast(I32), in0=gain_f[:].bitcast(I32), scalar1=23, scalar2=23,
                op0=ALU.logical_shift_right, op1=ALU.logical_shift_left,
            )
            nc.vector.tensor_scalar(out=expo[:], in0=frac[:], scalar1=0.0, scalar2=GAMMA, op0=ALU.mult, op1=ALU.add)
            nc.vector.tensor_copy(out=signs[:], in_=power[:])
            for c in range(G):
                cols = slice(8 * c, 8 * (c + 1))
                nc.gpsimd.tensor_tensor(out=lift[:, cols], in0=frac[:, cols], in1=expo[:, cols], op=ALU.pow)

        tcodes = {}

        def permute_transport(c, h):
            eng = nc.vector if PERM[c] == "V" else nc.gpsimd
            if h == 0:
                codes = work.tile([128, 16, 256], U8, align_bytes=64, name="codes")
                scales = work.tile([128, 2, 2, 4, 128], U8, align_bytes=64, name="scales")
                tcodes[c] = (codes, scales)
            codes, scales = tcodes[c]
            for g in range(2):
                i = 2 * g + h
                eng.tensor_copy(
                    out=codes[:, 4 * i : 4 * (i + 1), :].rearrange("p t (m b) -> p t m b", b=2),
                    in_=traws[c][:, g, 1024 * h : 1024 * (h + 1)].rearrange("p (m t b) -> p t m b", t=4, b=2),
                )
            if c == 0 and h == 0:
                split_gain()
            eng.tensor_copy(
                out=scales[:, :, h],
                in_=t_planes[:, 2048 * c : 2048 * (c + 1)].rearrange("p (g h m t) -> p h g t m", g=2, h=2, t=4)[:, h],
            )

        xs, pq = {}, {}

        def turn(u, rt):
            if rt == 0:
                x = work.tile([128, 2, N * 4], BF16, align_bytes=64, name="x", tag="quad", bufs=5)
                xs[u] = x
            xw = xs[u][:].rearrange("p g w -> p (g w)").bitcast(F32).rearrange("p (g r e) -> p g r e", g=2, e=2)
            tp = psum.tile([128, 4, 128], F32, name="tp", tag="bank")
            words = pats[u][:, rt, :].bitcast(F32)
            for g in range(2):
                for e in range(2):
                    nc.tensor.transpose(tp[:, 2 * g + e, :], words[:, 256 * g + e : 256 * (g + 1) : 2], ident[:])
            copy(EVAC[u][rt], xw[:, :, 128 * rt : 128 * (rt + 1), :], tp[:].rearrange("p (g e) r -> p g r e", g=2))

        def quantize_patterns(u, g):
            if g == 0:
                codes = work.tile([128, 2, N], U32, align_bytes=64, name="qcodes", tag="qcodes", bufs=4)
                scales = work.tile([128, 2, N], U8, align_bytes=64, name="qscales", tag="qscales", bufs=4)
                pq[u] = (codes, scales)
            codes, scales = pq[u]
            nc.vector.quantize_mx(out=codes[:, g, :].bitcast(E4M3), scales=scales[:, g, :], in_=xs[u][:, g, :])

        ms, ls = {}, {}

        def stage1(u, h, t):
            c = UNITS[u][0]
            tcode, tscale = tcodes[c]
            codes, scales = pq[u]
            if t == 0:
                m = work.tile([128, 4, N], F32, name="m", bufs=5)
                ms[u, h] = m
            acc = psum.tile([128, N], F32, name="acc", tag="bank")
            for g in range(2):
                nc.tensor.matmul_mx(
                    out=acc[:], lhsT=tcode[:, 8 * g + 4 * h + t, :].bitcast(E2M1), lhsT_scale=tscale[:, g, h, t],
                    rhs=codes[:, g, :].bitcast(E4M3), rhs_scale=scales[:, g, :], start=g == 0, stop=g == 1,
                )
            col = 8 * c + 4 * h + t
            nc.vector.tensor_scalar(
                out=ms[u, h][:, t, :], in0=acc[:], scalar1=BLACK, scalar2=lift[:, col : col + 1],
                op0=ALU.max, op1=ALU.mult,
            )

        def log(u, h):
            lg = work.tile([128, 2, N, 2], F32, name="lg", bufs=8)
            nc.scalar.activation(out=lg[:], in_=ms[u, h][:].rearrange("p (q e) n -> p q n e", e=2), func=ACT.Ln)
            ls[u, h] = lg

        ys, cq = {}, {}

        def exp(u, h, r0, r1):
            if h == 0 and r0 == 0:
                y = work.tile([128, 2, N, 4], BF16, align_bytes=64, name="y", tag="quad", bufs=5)
                ys[u] = y
            nc.scalar.activation(
                out=ys[u][:, h, r0:r1].rearrange("p n (q e) -> p n q e", e=2),
                in_=ls[u, h][:, :, r0:r1].rearrange("p q n e -> p n q e"), func=ACT.Exp, scale=1.0 / GAMMA,
            )

        def sign(eng, u, h, r0, r1):
            col = 8 * UNITS[u][0] + 4 * h
            y = ys[u][:, h, r0:r1]
            eng.tensor_tensor(
                out=y, in0=y, in1=signs[:, col : col + 4].unsqueeze(1).to_broadcast([128, r1 - r0, 4]), op=ALU.mult
            )

        def quantize_corrected(u, h, r0, r1):
            if h == 0 and r0 == 0:
                codes = work.tile([128, 2, N], U32, align_bytes=64, name="qcodes", tag="qcodes", bufs=4)
                scales = work.tile([128, 2, N], U8, align_bytes=64, name="qscales", tag="qscales", bufs=4)
                cq[u] = (codes, scales)
            codes, scales = cq[u]
            nc.vector.quantize_mx(
                out=codes[:, h, r0:r1].bitcast(E4M3), scales=scales[:, h, r0:r1],
                in_=ys[u][:, h, r0:r1].rearrange("p n t -> p (n t)"),
            )

        outs = {}

        def stage2(u, rt, stores):
            c, h = UNITS[u]
            codes, scales = cq[u]
            if rt == 0:
                o = work.tile([128, RT, V], F32, name="o", tag="io", bufs=3)
                outs[u] = o
            acc = psum.tile([128, V], F32, name="oacc", tag="bank")
            cols = slice(128 * rt, 128 * (rt + 1))
            for g in range(2):
                k = 2 * c + g
                nc.tensor.matmul_mx(
                    out=acc[:], lhsT=codes[:, g, cols].bitcast(E4M3), lhsT_scale=scales[:, g, cols],
                    rhs=e_words[:, 1024 * k : 1024 * (k + 1)].bitcast(E2M1),
                    rhs_scale=e_planes[:, 512 * k : 512 * (k + 1)], start=g == 0, stop=g == 1,
                )
            copy(OUT[u][rt], outs[u][:, rt, :], acc[:])
            if (rt + 1) % stores == 0:
                rows = slice(rt + 1 - stores, rt + 1)
                nc.sync.dma_start(
                    out=out[c, N * h : N * (h + 1), :].rearrange("(p r) v -> p r v", r=RT)[:, rows, :],
                    in_=outs[u][:, rows, :],
                )

        for rt in range(RT):
            turn(0, rt)
        permute_transport(0, 0)
        quantize_patterns(0, 0)
        quantize_patterns(0, 1)
        permute_transport(0, 1)
        for rt in range(RT):
            turn(1, rt)
        load_transport(2, [(0, 2048)])
        load_patterns(3, 2)
        load_encoder()
        for u in range(LAST + 1):
            if u in PERMAT:
                c = PERMAT[u]
                permute_transport(c, 0)
                permute_transport(c, 1)
            for h in range(2):
                for t in range(4):
                    stage1(u, h, t)
                    if u == 0 and h == 0 and t % 2:
                        quantize_patterns(1, t // 2)
                log(u, h)
                if u + 2 <= LAST:
                    turn(u + 2, 2 * h)
                    turn(u + 2, 2 * h + 1)
            if u + 2 <= LAST:
                quantize_patterns(u + 2, 0)
                quantize_patterns(u + 2, 1)
            if u + 4 <= LAST:
                load_patterns(u + 4, 2)
            if u == FIRST - 1:
                for v in range(FIRST):
                    for h in range(2):
                        exp(v, h, 0, N)
                        if v < GPSIGN:
                            for r0 in range(0, N, SIGNCHUNK):
                                sign(nc.gpsimd, v, h, r0, r0 + SIGNCHUNK)
        for u in range(FIRST, LAST):
            for h in range(2):
                exp(u, h, 0, N)
        for u in range(LAST):
            for h in range(2):
                if u >= GPSIGN:
                    sign(nc.vector, u, h, 0, N)
                if u:
                    stage2(u - 1, h, 2)
            for h in range(2):
                quantize_corrected(u, h, 0, N)
                if u:
                    stage2(u - 1, 2 + h, 2)
        for rt in range(RT):
            for h in range(2):
                exp(LAST, h, 128 * rt, 128 * (rt + 1))
        for rt in range(RT + 1):
            if rt < RT:
                stage2(LAST - 1, rt, 2)
                for h in range(2):
                    sign(nc.vector, LAST, h, 128 * rt, 128 * (rt + 1))
            if rt:
                for h in range(2):
                    quantize_corrected(LAST, h, 128 * (rt - 1), 128 * rt)
                stage2(LAST, rt - 1, 1)
